import numpy as np, ml_dtypes
CORES = [2,6,10,14,18,22,26,30]
N = 8
BF = ml_dtypes.bfloat16
W, S, M, CAP, RO, DX = 8192, 512, 16, 64, 4, 4
def places(g, w, k):
    u = np.add.reduce(w[..., :, None] * g, axis=-2) & 4095
    return ((u * u >> 5)[..., None, :] + k[..., :, None] * u[..., None, :]) & (W - 1)
def parts(rng):
    return (rng.integers(0, 256, (N, 8, 16, W), dtype=np.int32), rng.integers(0, 256, (N, 8, 16, S)), rng.integers(0, 256, (N, 8, 16, RO)),
            rng.integers(0, 3969, (N, 8, M)), rng.integers(620, 1000, (N, 8)))
def pack(x, g, w, k, t):
    return {"xs": x.reshape(N, 128, W).astype(np.float32).astype(BF), "gd": g.reshape(N, 128, S).astype(np.float32).astype(BF), "wt": w.reshape(N, 128, RO).astype(np.int32),
            "km": np.repeat(k, 16, axis=1).astype(np.int32), "th": np.repeat(t, 16, axis=1)[:, :, None].astype(np.int32)}
def plant(x, g, j, c, i, d):
    v = 255 - g[:, j]; n = np.arange(len(j)); a = v[i, n]
    v[i, n] = np.where(a < 128, a + d, a - d); x[:, c] = v
def lone(rng, x, g, w, k, s0, s1, lo, hi):
    c = places(g, w, k)[:, s0:s1]; m, j = np.nonzero((c >= lo) & (c < hi))
    if len(m):
        i = int(rng.integers(0, len(m))); x[:, c[m[i], j[i]]] = 255 - g[:, s0 + j[i]]
def setup_inputs(rng):
    x, g, w, k, t = parts(rng); h = rng.integers(0, 8)
    t[0, h] = 995; t[1, h] = 620; t[DX, h] = 620
    return pack(x, g, w, k, t)
def setup_inputs_room(rng):
    x, g, w, k, t = parts(rng); t = rng.integers(60, 129, (N, 8)); k = np.minimum(k | 1, 3967)
    for q in range(N):
        room = rng.permutation(np.array([0, 1, CAP - 1, CAP, CAP + 1, 2 * CAP, 0, CAP]))
        for h in range(8):
            c = places(g[q, h], w[q, h, :, 0], k[q, h])[rng.integers(0, M, S), np.arange(S)]
            o = rng.permutation(S); o = o[c[o] < W - 96]; first = np.unique(c[o], return_index=True)[1]
            o = o[np.sort(first)][:int(room[h])]; n = len(o)
            plant(x[q, h], g[q, h], o, c[o], rng.integers(0, 16, n), rng.integers(0, t[q, h], n))
    return pack(x, g, w, k, t)
def setup_inputs_ties(rng):
    x, g, w, k, t = parts(rng)
    w[:, :, 2, 0] = w[:, :, 1, 0]; g[:, :, 1] = np.minimum(g[:, :, 1], 254); g[:, :, 2] = np.maximum(g[:, :, 2], 1)
    for q in range(N):
        for h in (0, 2, 4, 6):
            n = int(rng.choice(np.array([CAP // 4, CAP // 2, CAP]))); t[q, h] = 3 if h == 2 * (q % 4) else rng.integers(1, 4)
            o = rng.permutation(S); a = np.minimum(o[:n], o[n:2 * n]); b = np.maximum(o[:n], o[n:2 * n]); e = o[2 * n:3 * n]
            kd = rng.integers(0, 4, n); kd[:4] = np.arange(4); s = (kd > 0).astype(np.int64)
            v = g[q, h][:, a].copy(); v[1] += s; v[2] -= s; g[q, h][:, b] = v
            c = places(g[q, h], w[q, h, :, 0], k[q, h])
            ca = c[rng.integers(0, M, n), a]; m = rng.integers(0, M, n); c1 = c[m, e]; c2 = c[(m + rng.integers(1, M, n)) % M, e]
            al = np.concatenate([ca, c1, c2]); one = np.bincount(al, minlength=W)[al] == 1
            pa = one[:n] & (ca < W - 96); pe = one[n:2 * n] & one[2 * n:]
            v = 255 - g[q, h][:, a]; v[1] -= ((kd == 1) | (kd == 2)).astype(np.int64); v[2] += (kd == 1).astype(np.int64); x[q, h][:, ca[pa]] = v[:, pa]
            i = rng.integers(0, 16, n); d = rng.integers(0, t[q, h], n)
            plant(x[q, h], g[q, h], e[pe], c1[pe], i[pe], d[pe]); plant(x[q, h], g[q, h], e[pe], c2[pe], i[pe], d[pe])
    a = int(rng.integers(0, S // 4)); b = a + int(rng.integers(1, S // 4))
    w[:, 1, :, 0] = 0; w[:, 1, 0, 0] = 1; k[:, 1, 0] = 0; k[:, 1, 1] = 3; t[:, 1] = 20
    g[:, 1, :, b] = g[:, 1, :, a].copy(); g[:, 1, 0, a] = 32; g[:, 1, 0, b] = 64
    x[:, 1, :, 128] = 255 - g[:, 1, :, a]; x[:, 1, 0, 128] = 207
    return pack(x, g, w, k, t)
def setup_inputs_ends(rng):
    x, g, w, k, t = parts(rng); o = rng.permutation(8); w[:, :, 0, 0] |= 1
    low = rng.integers(0, 192, (N, 4, W)); few = rng.integers(0, 64, (N, W)) == 0
    x[:, o[0], 0] = low[:, 0]; x[:, o[1], 0] = rng.integers(192, 256, (N, W))
    x[:, o[2], 0] = low[:, 1]; x[:, o[2], 0, 0] = 192; x[::2, o[2], 0, W - 1] = 255
    x[1::2, o[2], 0, W - 40] = 192; x[1::2, o[2], 0, W - 20] = 192
    x[:, o[3], 0, W // 2:] = low[:, 2, W // 2:]; x[:, o[4], 0] = np.where(few, 192, low[:, 3])
    x[:, o[6], 0, W - 81:] = low[:, 0, W - 81:]; x[:, o[7], 0, W - 81:] = low[:, 1, W - 81:]; x[:, o[7], 0, W - 4] = 192
    t[::2, o[0]] = 4080; t[1::2, o[0]] = 4; t[1::2, o[2]] = 4
    for q in range(1, N, 2):
        lone(rng, x[q, o[0]], g[q, o[0]], w[q, o[0], :, 0], k[q, o[0]], 0, S // 4, W // 2, W - 96)
        lone(rng, x[q, o[0]], g[q, o[0]], w[q, o[0], :, 1], k[q, o[0]], S // 4, S - 3 * CAP, 0, W // 4)
        lone(rng, x[q, o[2]], g[q, o[2]], w[q, o[2], :, 0], k[q, o[2]], 0, S, 0, W // 4)
    for q in range(N):
        for h in o[5:]:
            u = np.add.reduce(w[q, h, :, 0][:, None] * g[q, h], axis=0) & 4095; used = []
            for m, c in enumerate((W - 97, W - 96, 0)):
                for j in range(S):
                    if u[j] & 1 and j not in used:
                        v = int(u[j]); kk = (c - (v * v >> 5)) * pow(v, -1, W) % W
                        if kk <= 3968:
                            k[q, h, m] = kk; used.append(j)
                            plant(x[q, h], g[q, h], np.array([j]), np.array([c]), np.array([3 + m]), np.array([m])); break
    return pack(x, g, w, k, t)
def setup_inputs_alike(rng):
    x, g, w, k, t = parts(rng); o = rng.permutation(8)
    g[:, o[0]] = g[:, o[0], :, :1].copy()
    for q in range(N):
        c = places(g[q, o[0]], w[q, o[0], :, 0], k[q, o[0]])[:, 0]; m = np.flatnonzero(c < W - 96)[:1]
        plant(x[q, o[0]], g[q, o[0]], np.zeros(len(m), np.int64), c[m], m, np.full(len(m), 3))
    w[:, o[1]] = 0
    for q in range(N):
        e = np.arange(1, CAP + 1); d = np.append(e[::-1] if q % 2 == 0 else e, 0); n = np.arange(CAP + 1); i = rng.integers(0, 16, CAP + 1)
        v = np.repeat(255 - x[q, o[1], :, :1], CAP + 1, axis=1); a = v[i, n]
        v[i, n] = np.where(a < 128, a + d, a - d); g[q, o[1], :, :CAP + 1] = v
    k[:, o[2]] = k[:, o[2], :1].copy()
    g[:, o[3]] = g[:, o[3]][:, :, rng.integers(0, 4, S)]
    b = x[:, o[4], :, :8].copy(); b[:, 0, 0] = 200
    x[:, o[4]] = b[:, :, rng.integers(0, 8, W)]; g[:, o[4]] = 255 - b[:, :, rng.integers(0, 8, S)]
    k[:, o[5]] = rng.choice(np.array([0, 1, 3968]), (N, M))
    x[:, o[6]] = 255 * rng.integers(0, 2, (N, 16, W)); g[:, o[6]] = 255 * rng.integers(0, 2, (N, 16, S))
    w[:, o[7], :, 0] = 0; w[:, o[7], 0, 0] = 1; k[:, o[7]] = rng.integers(0, 8, (N, M)); t[:, o[7]] = 4080
    g[:, o[7], 0] = np.minimum(g[:, o[7], 0], 254); g[:, o[7], 0, S - 1] = 255
    for q in range(N):
        c = int(places(g[q, o[7]], w[q, o[7], :, 0], k[q, o[7]])[0, S - 1]); x[q, o[7], :, c] = 255 - g[q, o[7], :, S - 1]
    return pack(x, g, w, k, t)
def setup_inputs_spread(rng):
    x, g, w, k, t = parts(rng)
    def uneven(n):
        v = np.minimum((np.exp2(8 * rng.random((N, 8, 1, n))) * rng.random((N, 8, 16, n))).astype(np.int64), 255)
        return np.where(rng.random((N, 8, 1, n)) < 0.5, v, 255 - v)
    x = uneven(W); g = uneven(S)
    w = np.minimum(np.exp2(8 * rng.random(w.shape)).astype(np.int64), 255); k = np.minimum(np.exp2(12 * rng.random(k.shape)).astype(np.int64), 3968)
    t = np.minimum(np.maximum(np.exp2(12 * rng.random((N, 8))).astype(np.int64), 1), 4080); t[:, rng.integers(0, 8)] = rng.integers(1500, 2500, N)
    return pack(x, g, w, k, t)
def check_inputs(d):
    bad = []
    for n, lo, hi in (("xs", 0, 255), ("gd", 0, 255), ("wt", 0, 255), ("km", 0, 3968), ("th", 1, 4080)):
        a = np.asarray(d[n]).astype(np.float64)
        if not np.all((a >= lo) & (a <= hi) & (np.floor(a) == a)): bad.append("range of " + n)
    for n in ("km", "th"):
        a = np.asarray(d[n]).reshape(N, 8, 16, -1)
        if np.any(a != a[:, :, :1]): bad.append("rows of a group alike in " + n)
    return bad
def reference(xs, gd, wt, km, th):
    x = xs.astype(np.float32).astype(np.int32).reshape(N, 8, 16, W); g = gd.astype(np.float32).astype(np.int32).reshape(N, 8, 16, S)
    w = wt.astype(np.int64).reshape(N, 8, 16, RO); k = km.astype(np.int64).reshape(N, 8, 16, M)[:, :, 0]; t = th.astype(np.int64).reshape(N, 8, 16)[:, :, 0]
    log = np.zeros((N, 8, W), np.int64); place = np.arange(W); slot = np.arange(S); rows = np.arange(8)[:, None]
    for rnd in range(RO):
        cuts = []; gives = []; nx = []
        for a in range(N):
            c = places(g[a], w[a, :, :, rnd], k[a])
            v = np.take_along_axis(x[a], c.reshape(8, 1, M * S), 2).reshape(8, 16, M, S)
            D = np.add.reduce(np.abs(g[a][:, :, None, :] + v - 255), axis=1)
            m = np.argmin(D, axis=1)[:, None]
            D = np.take_along_axis(D, m, 1)[:, 0].astype(np.int64); c = np.take_along_axis(c, m, 1)[:, 0]
            fit = (D < t[a][:, None]) & (c < W - 96)
            cand = fit & (np.add.accumulate(fit.astype(np.int64), axis=1) <= CAP)
            key = D * S + slot; low = np.full((8, W), 2 ** 40, np.int64)
            np.minimum.at(low, (rows, c), np.where(cand, key, 2 ** 40))
            cut = cand & (np.take_along_axis(low, c, 1) == key)
            ok = (x[a][:, 0] >= 192) & (x[a][:, 0] <= 255)
            U = np.minimum.accumulate(np.where(ok, place, W - 1)[:, ::-1], axis=1)[:, ::-1]
            e1 = np.take_along_axis(U, np.minimum(c + 16, W - 1), 1); e2 = np.take_along_axis(U, np.minimum(e1 + 8, W - 1), 1)
            gives.append([np.maximum(255 - np.take_along_axis(x[a], e[:, None, :], 2), 0) for e in (np.minimum(c + 10, W - 1), e1, e2)])
            reach = np.full((8, W), -1, np.int64); np.maximum.at(reach, (rows, c), np.where(cut, e2, -1))
            gone = np.maximum.accumulate(reach, axis=1) >= place
            log[a] = np.where(gone & (log[a] == 0), rnd + 1, log[a])
            nx.append(np.where(gone[:, None, :], np.int32(512), x[a])); cuts.append(cut)
        ng = []
        for a in range(N):
            p, q = a ^ 1, a ^ DX
            every = np.concatenate([gives[p][0], gives[q][1], gives[q][2], g[a], g[a]], axis=2)
            there = np.concatenate([cuts[p], cuts[q], cuts[q], ~cuts[a], cuts[a]], axis=1)
            o = np.argsort(~there, axis=1, kind="stable")[:, :S]
            ng.append(np.take_along_axis(every, o[:, None, :], 2))
        x = np.stack(nx); g = np.stack(ng)
    return {"yg": g.reshape(N, 128, S).astype(np.float32).astype(BF), "yc": log.astype(np.float32)}

from concourse.mybir import AluOpType as O, AxisListType, ActivationFunctionType as F

RO = 4
QW = 784
QG = 208
DW = 976
BIG = 1.0e9

_f = "x0c:512b okl:512 oks:512 Ut:512 RV1:512b SG:2560b Yt:512 Yu:512 idf:128 idb:128b BM:128b BMgf:8 tri:128b oneb:512b onef:512 O16:16b"
_f += " tri2:128 BO2:128 id2:64 maskJ:512 i64b:64b i64f:64 mW:64 t32:32 z16:128 rs16:512 rs64:256 Kpat:512b Mpat:512b c16:128b c16f:128 thr:1 thS:32"
_f += " Bpat:128b TriB:128b cm:128 Pm:128b Jm:128b pi:1i pj:1i rcol:1 b512:1 acol:1 iW:32 dW:4 aW:8 i512:512 rself:128 rselb:128b kA:16i kB:16i kAf:16 kBf:16"
_f += " iM:16 slS:32i slL:32i tA:128 tB:128 X:8192b Urep:8256 A0:8192 Ab:8192b Gr0:1024b Gr1:1024b xs2:1024b wti:4i kmi:16i thi:1i wf:4 kf:16 Lw:2048b Lsel:2048b"
_f += " Wf:8b Wff:8 ui:64i U:64i sq:64i Fi:64i UF:64 FF:64 UU:64 T0:256i T1:256i T1f:256 OT0:256u OT1:256u KS0:512 KS1:512 Ki:64i kp:64i pr:64 tt:32i tf:32 tc:32i CD:64i CDl:64i"
_f += " VL:192b f1:32 f2:32 fit:32b rsel:32 OH:2048b Ls:24 cds:12 Vp:4 DG:512 EQ:256 SC:256 vm:4 win:4 E5:4 OE:264 rid:4 tmA:128 tmB:128 EW:8i cW:4i s1:8i tW:8 isl:4 q1:4 q2:4 q3:4"
_f += " OFF:24u OFC:4u OFD:4u UG:128 xg:192b yv:192b mk:192b mP:72b mT:136b PL:8i hiI:8i loI:8i hiF:8 loF:8 HH:1024b sgn:4096b c511:1b bs:1 bA:1 bB:1 Dw:976b DS:512b sN:2b A1:1 mi:192 MI:32u"
_f += " tot:1 dg:128 cmx:128 cry:1 Gn:512b"
_dt = {"b": "bfloat16", "i": "int32", "u": "uint16"}
_pool, _where, SCRATCH = {}, {}, {}
for _x in _f.split():
    _n, _c = _x.split(":")
    _d = _dt.get(_c[-1], "float32")
    _c = int(_c if _d == "float32" else _c[:-1])
    if _c <= 264 and _n not in ("mP", "mT"):
        _p = "pool_" + _d
        _where[_n] = (_p, _pool.get(_p, 0), _c)
        _pool[_p] = _pool.get(_p, 0) + (_c + 15) // 16 * 16
        SCRATCH[_p] = ("sbuf", [128, _pool[_p]], _d)
    else:
        _where[_n] = (_n, 0, _c)
        SCRATCH[_n] = ("sbuf", [128, _c], _d)
for _t in range(RO):
    SCRATCH["Q%d" % _t] = ("sbuf", [128, QW], "bfloat16")
    _where["Q%d" % _t] = ("Q%d" % _t, 0, QW)
for _t in range(8):
    SCRATCH["B%d" % _t] = ("psum", [128, 512], "float32")
    _where["B%d" % _t] = ("B%d" % _t, 0, 512)
NDMA = 48
SEMAPHORES = ["sv", "ss", "st", "sg"] + ["d%d" % _t for _t in range(NDMA)]
for _t in range(RO):
    SEMAPHORES += ["aP%d" % _t, "aT%d" % _t, "lP%d" % _t, "lT%d" % _t]


def rank_program(g, core, T, topo):
    rank = T.rank_of(core)
    if rank is None:
        return
    queues = {"v": g.vector, "s": g.scalar, "t": g.tensor, "g": g, "y": g.sync}
    own = {"v": "sv", "s": "ss", "t": "st", "g": "sg"}
    count, log = {}, {}
    known = {q: {} for q in queues}

    def A(n, lo=0, hi=None, st=1, p0=0, p1=128, pst=1):
        p, o, c = _where[n]
        hi = c if hi is None else hi
        hi = min(hi, lo + (hi - lo - 1) // st * st + 1)
        ap = T[p][p0:p1:pst, o + lo:o + hi:st] if (pst != 1 or st != 1) else T[p][p0:p1, o + lo:o + hi]
        return (ap, [(p, o + lo, o + hi, st, p0, p1)])

    def IX(win, off):
        return (win[0].indirect(off[0]), win[1] + off[1])

    def hit(a, b):
        if a[1] >= b[2] or b[1] >= a[2] or a[4] >= b[5] or b[4] >= a[5]:
            return False
        return not (a[3] == b[3] and a[3] > 1 and (a[1] - b[1]) % a[3])

    def need(q, reads, writes):
        w = {}
        for regs, isw in ((reads, False), (writes, True)):
            for r in regs:
                bank = r[0][0] == "B" and r[0][1:].isdigit()
                for (r2, w2, q2, sem, n, snap) in log.get(r[0], []):
                    if q2 == q and q2 in own:
                        if not (isw or w2) or not hit(r, r2) or (isw and q == "t"):
                            continue
                    elif not bank and (not (isw or w2) or not hit(r, r2)):
                        continue
                    if known[q].get(sem, 0) < n and w.get(sem, (0,))[0] < n:
                        w[sem] = (n, snap)
        for sem in sorted(w, key=lambda s: -len(w[s][1])):
            n, snap = w[sem]
            if known[q].get(sem, 0) >= n:
                continue
            queues[q].wait_ge(T.sem[sem], n)
            for k in snap:
                known[q][k] = max(snap[k], known[q].get(k, 0))
            known[q][sem] = n

    def note(q, reads, writes, sem, n, snap):
        for regs, isw in ((reads, False), (writes, True)):
            for r in regs:
                L = log.setdefault(r[0], [])
                if isw:
                    L[:] = [e for e in L if not (e[0][1] >= r[1] and e[0][2] <= r[2] and r[3] == 1 and e[0][4] >= r[4] and e[0][5] <= r[5])]
                else:
                    L[:] = [e for e in L if not (e[2] == q and not e[1] and e[0] == r and q in own)]
                L.append((r, isw, q, sem, n, snap))

    def rg(xs):
        return [r for x in xs if isinstance(x, tuple) for r in x[1]]

    def ap(x):
        return x[0] if isinstance(x, tuple) else x

    def run(q, outs, ins, f):
        r, w, s = rg(ins), rg(outs), own[q]
        need(q, r, w)
        count[s] = count.get(s, 0) + 1
        f().then_inc(T.sem[s], 1)
        note(q, r, w, s, count[s], dict(known[q]))

    V, SE, PE = g.vector, g.scalar, g.tensor

    def cp(o, i):
        run("v", [o], [i], lambda: V.tensor_copy(ap(o), ap(i)))

    def sct(win, off, i):
        run("v", [win], [off, i], lambda: V.tensor_copy(win[0].indirect(off[0]), ap(i)))

    def tt(o, a, b, op):
        run("v", [o], [a, b], lambda: V.tensor_tensor(ap(o), ap(a), ap(b), op))

    def ts(o, a, s1, op0, s2=None, op1=None):
        if op1 is None:
            run("v", [o], [a, s1], lambda: V.tensor_scalar(ap(o), ap(a), ap(s1), None, op0))
        else:
            run("v", [o], [a, s1, s2], lambda: V.tensor_scalar(ap(o), ap(a), ap(s1), ap(s2), op0, op1))

    def scan(o, a, b, init, op0, op1):
        run("v", [o], [a, b, init], lambda: V.tensor_tensor_scan(ap(o), ap(a), ap(b), ap(init), op0, op1))

    def ms(o, c):
        run("v", [o], [], lambda: V.memset(ap(o), c))

    def act(o, i, f, bias=None, scale=None):
        kw = {}
        if bias is not None:
            kw["bias"] = ap(bias)
        if scale is not None:
            kw["scale"] = ap(scale)
        run("s", [o], [i, bias, scale], lambda: SE.activation(ap(o), ap(i), f, **kw))

    def mm(o, l, r, start=True, stop=True):
        run("t", [o], [l, r], lambda: PE.matmul(ap(o), ap(l), ap(r), start, stop))

    def iota(o, pat, base, ch, small=True):
        kw = {"allow_small_or_imprecise_dtypes": True} if small else {}
        run("g", [o], [], lambda: g.iota(ap(o), pat, base, ch, **kw))

    def sel(o, i, pat, op, base, ch):
        run("g", [o], [i], lambda: g.affine_select(ap(o), ap(i), pat, op, 0.0, base, ch))

    nd = [0]

    def dma(q, o, i):
        r, w = rg([i]), rg([o])
        need(q, r, w)
        s = "d%d" % nd[0]
        nd[0] += 1
        queues[q].dma_start(ap(o), ap(i)).then_inc(T.sem[s], 16)
        count[s] = 16
        note("d" + s, r, w, s, 16, dict(known[q]))

    dma("y", A("Q0", QG, QG + 512), (T.gd[:, :], []))
    dma("y", A("wti"), (T.wt[:, :], []))
    dma("y", A("kmi"), (T.km[:, :], []))
    dma("y", A("x0c"), (T.xs[0:128:16, :], []))
    dma("y", A("thi"), (T.th[:, :], []))
    dma("y", A("X"), (T.xs[:, :], []))
    o128 = A("oneb", 0, 128)

    def weights(t):
        act(A("Wff"), A("BMgf"), F.Copy, None, A("wf", t, t + 1))
        act(A("Wf"), A("BMgf"), F.Copy, None, A("wf", t, t + 1))
        for q in range(8):
            act(A("Lw", 16 * q, 16 * q + 1936, 129), A("oneb", 0, 16), F.Copy, None, A("Wff", q, q + 1))

    def consts0():
        ms(A("oneb"), 1.0)
        sel(A("BM"), o128, [[-16, 8], [0, 16]], O.is_ge, 0, 1)
        sel(A("BM"), A("BM"), [[16, 8], [0, 16]], O.is_ge, 15, -1)
        iota(A("pi"), [[0, 1]], 0, 1, False)
        iota(A("iM"), [[64, 16]], 0, 0)
        ms(A("Lw"), 0.0)
        ms(A("onef"), 1.0)
        cp(A("wf"), A("wti"))
        cp(A("BMgf"), A("BM", 0, 128, 16))
        weights(0)
        cp(A("kf"), A("kmi"))

    def consts1():
        ms(A("c16"), 0.0625)
        ms(A("rs16"), 0.0)
        ms(A("rs16", 0, 512, 16), BIG)
        ts(A("O16", 0, 16, 2), A("BMgf"), 1024.0, O.mult)
        ts(A("O16", 1, 16, 2), A("BMgf"), 1024.0, O.mult)
        ts(A("kA"), A("kmi"), 6, O.logical_shift_right)
        ts(A("kB"), A("kmi"), 63, O.bitwise_and)
        cp(A("kAf"), A("kA"))
        cp(A("kBf"), A("kB"))
        for q in range(8):
            m = A("BMgf", q, q + 1)
            act(A("Kpat", q * 32, q * 32 + 16), A("kAf"), F.Copy, None, m)
            act(A("Kpat", q * 32 + 16, q * 32 + 32), A("kBf"), F.Copy, None, m)
            act(A("Mpat", q * 32, q * 32 + 16), A("iM"), F.Copy, None, m)
            act(A("Mpat", q * 32 + 16, q * 32 + 32), A("iM"), F.Copy, None, m)
        act(A("Kpat", 256, 512), A("Kpat", 0, 256), F.Copy)
        act(A("Mpat", 256, 512), A("Mpat", 0, 256), F.Copy)

    def consts2():
        sel(A("idf"), A("onef", 0, 128), [[-1, 128]], O.is_equal, 0, 1)
        sel(A("Pm"), o128, [[-16, 8], [1, 16]], O.is_equal, -15, 1)
        sel(A("Jm"), o128, [[1, 128]], O.is_equal, -127, 1)
        iota(A("i512"), [[1, 512]], 0, 0)
        sel(A("cm"), A("onef", 0, 128), [[-1, 128]], O.is_gt, 0, 1)
        sel(A("tri"), o128, [[1, 128]], O.is_ge, 0, -1)
        sel(A("tB"), A("onef", 0, 128), [[1, 128]], O.is_gt, 0, -1)
        iota(A("i64f"), [[1, 64]], 1, 0)
        iota(A("tA"), [[0, 8], [1, 16]], 5, 0)
        iota(A("iW"), [[16, 32]], 0, 0)
        iota(A("dW"), [[16, 4]], 706, 0)
        iota(A("aW"), [[1, 2], [16, 4]], 0, 0)
        iota(A("slS"), [[128, 4], [0, 8]], 1, 1, False)
        iota(A("Urep"), [[0, 8256]], 0, 0)
        iota(A("Dw"), [[0, DW]], 0, 0)
        ms(A("bA"), 191.5)
        ms(A("bB"), -256.0)
        act(A("SG", 2048, 2560), A("x0c"), F.Sign, A("bA"), -1.0)
        act(A("idb"), A("idf"), F.Copy)
        act(A("Jm"), A("Jm"), F.Copy, None, -16384.0)
        ts(A("pj"), A("pi"), 15, O.bitwise_and)
        cp(A("rcol"), A("pj"))
        ts(A("b512"), A("rcol"), 512.0, O.mult)
        ts(A("pj"), A("pi"), 63, O.bitwise_and)
        ts(A("acol"), A("pj"), -262144.0, O.add)
        tt(A("cm"), A("cm"), A("BM"), O.mult)

    def consts3():
        act(A("Lsel"), A("Lw"), F.Copy, None, 0.0)
        for q in range(8):
            act(A("Lsel", 16 * q, 16 * q + 1936, 129), A("c16", 0, 16), F.Copy, None, A("BMgf", q, q + 1))
        act(A("i64b"), A("i64f"), F.Copy)
        tt(A("id2"), A("idf", 0, 64), A("idf", 64, 128), O.add)
        tt(A("t32"), A("id2", 0, 32), A("id2", 32, 64), O.add)
        for k in range(4):
            tt(A("mW", 16 * k, 16 * k + 16), A("t32", 0, 16), A("t32", 16, 32), O.add)
        ms(A("c16f"), 0.0625)
        ms(A("z16"), 1.0)
        ms(A("z16", 0, 128, 16), 0.0)
        ms(A("rs64"), -BIG)
        ms(A("rs64", 0, 256, 64), BIG)
        cp(A("tri2"), A("tri"))
        ms(A("tri2", 64, 128, 1, 0, 64), 0.0)
        ms(A("BO2"), 0.0)
        ms(A("BO2", 0, 64, 1, 0, 64), 1.0)
        ms(A("BO2", 64, 128, 1, 64, 128), 1.0)
        ms(A("maskJ"), 0.0)
        for j in range(4):
            for h in range(2):
                c = j * 128 + (2 * j + h) * 16
                ms(A("maskJ", c, c + 16, 1, 64 * h, 64 * h + 64), 1.0)
        ts(A("bs"), A("rcol"), 0.0, O.is_equal)
        ts(A("rself"), A("BM"), A("bs"), O.mult)
        cp(A("rselb"), A("rself"))
        tt(A("tA"), A("tA"), A("BM"), O.mult)
        ts(A("Bpat"), A("tA"), -5.0, O.add)
        tt(A("tA"), A("tB"), A("tri"), O.add)
        tt(A("TriB"), A("tA"), A("BM"), O.mult)
        ts(A("iW"), A("iW"), A("rcol"), O.add)
        ts(A("dW"), A("dW"), A("rcol"), O.add)
        ts(A("aW"), A("aW"), A("rcol"), O.add)
        ts(A("slL"), A("slS"), 63, O.bitwise_and)
        cp(A("VL", 160, 192), A("slL"))
        tt(A("VL", 64, 96), A("slS"), A("slL"), O.subtract)
        ms(A("mP"), 0.0)
        ms(A("mT"), 0.0)
        ms(A("OE"), 0.0)
        cp(A("thr"), A("thi"))
        ts(A("tA", 0, 8), A("BMgf"), A("thr"), O.mult)
        mm(A("B6", 0, 8), A("c16f"), A("tA", 0, 8))
        for b in range(4):
            cp(A("thS", 8 * b, 8 * b + 8), A("B6", 0, 8))

    def p1a(t, ch):
        bank, Q, o = "B2" if ch == 0 else "B4", "Q%d" % t, QG + 256 * ch
        w, s = (0, 16) if ch == 0 else (16, 0)
        for r in range(16):
            mm(A(bank, w, w + 16), A("Lw", r * 128, r * 128 + 128), A(Q, o + r, o + 256, 16), r == 0, r == 15)
        for b in range(2):
            mm(A(bank, s + 8 * b, s + 8 * b + 8), A(Q, o + 128 * b, o + 128 * b + 128), A("Wf"))

    def p1b(ch):
        a, b = 32 * ch, 32 * ch + 32
        cp(A("ui", a, b), A("B2" if ch == 0 else "B4", 0, 32))
        ts(A("U", a, b), A("ui", a, b), 4095, O.bitwise_and)
        tt(A("sq", a, b), A("U", a, b), A("U", a, b), O.mult)
        cp(A("UF", a, b), A("U", a, b))
        ts(A("Fi", a, b), A("sq", a, b), 5, O.logical_shift_right)
        cp(A("FF", a, b), A("Fi", a, b))

    def lists(ch):
        for b in range(16):
            k = b + 48 * ch
            u, f = A("UF", k, k + 1), A("FF", k, k + 1)
            if ch:
                act(A("T1f", b, 256, 16), A("kf"), F.Identity, f, u)
            else:
                ts(A("T0", b, 256, 16), A("kf"), u, O.mult, f, O.add)

    def lists2(ch):
        n = "T%d" % ch
        if ch:
            cp(A("T1"), A("T1f"))
        ts(A(n), A(n), 8191, O.bitwise_and)
        cp(A("O" + n), A(n))

    def reps0(t):
        for k in range(4):
            act(A("Gr0", 256 * k, 256 * k + 256), A("Q%d" % t, QG, QG + 256), F.Copy)

    def reps1(t):
        for k in range(4):
            dma("y", A("Gr1", 256 * k, 256 * k + 256), A("Q%d" % t, QG + 256, QG + 512))

    def patterns(ch):
        mm(A("B%d" % ch), A("c16"), A("Kpat"), True, False)
        mm(A("B%d" % ch), A("c16"), A("Mpat"), False, False)

    def sums(ch, m0, m1, last):
        for m in range(m0, m1):
            for b in range(2):
                a = ch * 4096 + m * 256 + b * 128
                mm(A("B%d" % ch, b * 256 + m, b * 256 + m + 241, 16), A("Ab", a, a + 128), A("O16"), False, last and m == m1 - 1 and b == 1)

    def gather(ch, m0, m1, last=False):
        n, o = (m1 - m0) * 256, ch * 4096 + m0 * 256
        tt(A("A0", o, o + n), IX(A("X"), A("OT%d" % ch, m0 * 16, m1 * 16)), A("Gr%d" % ch, 0, n), O.add)
        act(A("Ab", o, o + n), A("A0", o, o + n), F.Abs, -255.0)
        sums(ch, m0, m1, last)

    def sgather(m0, bank, k):
        act(A("xs2", 512 * k, 512 * k + 512), IX(A("X"), A("OT1", m0 * 16, m0 * 16 + 32)), F.Copy)
        mm(A(bank), A("idb"), A("xs2", 512 * k, 512 * k + 512), True, False)
        mm(A(bank), A("idb"), A("Gr1", 0, 512), False, True)

    def sgather2(m0, bank):
        o = 4096 + m0 * 256
        act(A("Ab", o, o + 512), A(bank), F.Abs, -255.0)
        sums(1, m0, m0 + 2, False)

    def lowest(ch):
        scan(A("KS%d" % ch), A("rs16"), A("B%d" % ch), 0.0, O.max, O.min)
        cp(A("Ki", 32 * ch, 32 * ch + 32), A("KS%d" % ch, 15, 512, 16))

    def decode():
        ts(A("kp"), A("Ki"), 63, O.bitwise_and)
        ts(A("CD", 32, 64), A("Ki", 0, 64, 2), 10, O.logical_shift_right)
        tt(A("pr"), A("kp"), A("UU"), O.mult)
        tt(A("f1"), A("CD", 32, 64), A("thS"), O.is_lt)
        tt(A("tf"), A("pr", 0, 64, 2), A("pr", 1, 64, 2), O.add)
        tt(A("tc"), A("tf"), A("FF", 16, 48), O.add)
        ts(A("tt"), A("tc"), 8191, O.bitwise_and)
        ts(A("CD", 0, 32), A("tt"), 64.0, O.add)
        ts(A("f2"), A("tt"), 8096.0, O.is_lt)
        tt(A("fit"), A("f1"), A("f2"), O.mult)

    def choose():
        mm(A("B2", 0, 32), A("tri"), A("fit"), True, False)
        mm(A("B2", 8, 32), o128, A("fit", 0, 24), False, False)
        mm(A("B2", 16, 32), o128, A("fit", 0, 16), False, False)
        mm(A("B2", 24, 32), o128, A("fit", 0, 8), False, True)
        ts(A("CDl"), A("CD"), 63, O.bitwise_and)
        tt(A("VL", 0, 64), A("CD"), A("CDl"), O.subtract)
        cp(A("VL", 96, 160), A("CDl"))
        tt(A("rsel"), A("B2", 0, 32), A("fit"), O.mult)
        for q in range(8):
            for b in range(4):
                c = b * 8 + q
                ts(A("OH", c * 64, c * 64 + 64), A("i64b"), A("rsel", c, c + 1), O.is_equal)
                h, j = q % 2, q // 2
                mm(A("B3", j, j + 21, 4, 64 * h, 64 * h + 64), A("OH", c * 64, c * 64 + 64), A("VL", c, c + 161, 32), b == 0, b == 3)

    def resolve():
        cp(A("Ls"), A("B3", 0, 24))
        tt(A("cds"), A("Ls", 0, 12), A("Ls", 12, 24), O.add)

        def diag(to, col):
            for j in (2, 3):
                act(A("DG", to + 64 * j, to + 64 * j + 64), A("id2"), F.Copy, None, A(col, j, j + 1))
            for j in (0, 1):
                ts(A("DG", to + 64 * j, to + 64 * j + 64), A("id2"), A(col, j, j + 1), O.mult)

        diag(0, "cds")
        mm(A("B4", 0, 256), A("BO2"), A("DG", 0, 256))
        ts(A("Vp"), A("cds", 4, 8), 64.0, O.mult, A("acol"), O.add)
        diag(256, "Vp")
        mm(A("B5", 0, 256), A("BO2"), A("DG", 256, 512))
        ts(A("E5"), A("cds", 0, 4), 1024.0, O.mult)
        tt(A("E5"), A("E5"), A("cds", 8, 12), O.add)
        ts(A("vm"), A("cds", 0, 4), 64.0, O.is_ge)
        for j in range(4):
            ts(A("EQ", 64 * j, 64 * j + 64), A("B4", 64 * j, 64 * j + 64), A("cds", j, j + 1), O.is_equal)
        tt(A("EQ"), A("EQ"), A("B5", 0, 256), O.mult)
        scan(A("SC"), A("rs64"), A("EQ"), 0.0, O.max, O.min)
        tt(A("win"), A("SC", 63, 256, 64), A("Vp"), O.is_equal)
        tt(A("OE", 65, 264, 66), A("win"), A("vm"), O.mult)
        mm(A("B3", 32, 36), A("tri2"), A("OE", 65, 264, 66))
        tt(A("rid"), A("B3", 32, 36), A("OE", 65, 264, 66), O.mult)
        for j in range(4):
            ts(A("OE", 66 * j, 66 * j + 64), A("i64f"), A("rid", j, j + 1), O.is_equal, A("E5", j, j + 1), O.mult)
            mm(A("B6", 0, 66), A("maskJ", 128 * j, 128 * j + 128), A("OE", 66 * j, 66 * j + 66), j == 0, j == 3)

    def wrap(src, src2=None):
        tt(A("tmA", 0, 64), src, A("mW"), O.mult)
        if src2 is not None:
            tt(A("tmA", 64, 128), src2, A("mW"), O.mult)
        n = 64 if src2 is None else 128
        scan(A("tmB", 0, n), A("z16", 0, n), A("tmA", 0, n), 0.0, O.mult, O.add)
        return A("tmB", 15, n, 16)

    def send(t, what):
        dst = T.cores[rank ^ (1 if what == "P" else 4)]
        e = topo.engines(core, dst)
        e = e[8:16] if what == "P" else e[:8]
        rid, pid, _ = topo.addr(dst)
        src = A("m" + what)
        land = A("Q%d" % t, 0, 72) if what == "P" else A("Q%d" % t, 72, QG)
        need("g", src[1], [])
        la, aa = "l%s%d" % (what, t), "a%s%d" % (what, t)
        g.remote_dma(out_ap=land[0], in_ap=src[0], remote_sem=T.sem[aa], local_sem=T.sem[la], pid=pid, routing_id=rid, dma_engine_mask=sum(1 << x for x in e))
        count[la] = count[aa] = len(e)
        note("r", src[1], [], la, len(e), dict(known["g"]))
        note("r", [], land[1], aa, len(e), {})

    def marks(k):
        ts(A("hiI", k, k + 4), A("PL", k, k + 4), 9, O.arith_shift_right)
        ts(A("loI", k, k + 4), A("PL", k, k + 4), 511, O.bitwise_and)
        ts(A("loF", k, k + 4), A("loI", k, k + 4), -1.0, O.mult, 0.5, O.add)
        cp(A("hiF", k, k + 4), A("hiI", k, k + 4))
        for i in range(k, k + 4):
            act(A("sgn", 512 * i, 512 * i + 512), A("i512"), F.Sign, A("loF", i, i + 1))

    def blocks(k):
        for i in range(k, k + 4):
            ts(A("HH", 128 * i, 128 * i + 128), A("Bpat"), A("hiF", i, i + 1), O.is_equal, 4096.0 if k == 0 else -4096.0, O.mult)

    def cover(k):
        for i in range(k, k + 4):
            mm(A("B5"), A("HH", 128 * i, 128 * i + 128), A("sgn", 512 * i, 512 * i + 512), i == 0, i == 7)

    def give(t):
        n = A("B6", 65, 66)
        cp(A("EW"), wrap(A("B6", 0, 64), A("B6", 1, 65)))
        ts(A("cW"), A("EW", 0, 4), 10, O.logical_shift_right)
        ts(A("OFF", 4, 8), A("cW"), -1.0, O.mult, 8239.0, O.add)
        cp(A("UG", 0, 64), IX(A("Urep"), A("OFF", 4, 8)))
        mm(A("B0", 0, 64), A("rself"), A("UG", 0, 64))
        act(A("mP", 64, 65), n, F.Copy)
        act(A("mP", 65, 66), n, F.Copy, 72.0, -1.0)
        act(A("mT", 128, 129), n, F.Copy)
        act(A("mT", 129, 130), n, F.Copy, 64.0, -1.0)
        act(A("mT", 130, 131), n, F.Copy, 72.0, -1.0)
        ts(A("OFF", 0, 4), A("cW"), -54.0, O.add, 0.0, O.max)
        cp(A("xg", 0, 64), IX(A("X"), A("OFF", 0, 4)))
        mm(A("B7", 0, 64), A("rselb"), A("xg", 0, 64))
        ts(A("yv", 0, 64), A("xg", 0, 64), -1.0, O.mult, 255.0, O.add)
        ts(A("PL", 0, 4), A("cW"), -64.0, O.add)
        marks(0)
        e1 = wrap(A("B0", 0, 64))
        ts(A("OFF", 16, 20), e1, -8.0, O.add, 0.0, O.max)
        cp(A("UG", 64, 128), IX(A("Urep"), A("OFF", 16, 20)))
        mm(A("B1", 0, 64), A("rself"), A("UG", 64, 128))
        ts(A("OFF", 8, 12), e1, -1.0, O.mult, 8191.0, O.add)
        ts(A("mk", 0, 64), A("B7", 0, 64), 256.0, O.is_lt)
        tt(A("mP", 0, 64), A("mk", 0, 64), A("yv", 0, 64), O.mult)
        send(t, "P")
        e2 = wrap(A("B1", 0, 64))
        ts(A("OFF", 12, 16), e2, -1.0, O.mult, 8191.0, O.add)
        cp(A("xg", 64, 192), IX(A("X"), A("OFF", 8, 16)))
        mm(A("B7", 64, 192), A("rselb"), A("xg", 64, 192))
        ts(A("yv", 64, 192), A("xg", 64, 192), -1.0, O.mult, 255.0, O.add)
        ts(A("PL", 4, 8), e2, -1.0, O.mult, 8192.0, O.add)
        ts(A("mk", 64, 192), A("B7", 64, 192), 256.0, O.is_lt)
        tt(A("mT", 0, 128), A("mk", 64, 192), A("yv", 64, 192), O.mult)
        send(t, "T")
        marks(4)
        blocks(0)
        cover(0)
        blocks(4)
        cover(4)

    def order(t):
        ts(A("s1"), A("EW"), 1023, O.bitwise_and)
        tt(A("tW"), A("s1"), A("aW"), O.subtract)
        ts(A("OFC"), A("s1", 0, 4), -1.0, O.add, 0.0, O.max)
        ts(A("q1"), A("tW", 0, 4), 0.0, O.max)
        tt(A("isl"), A("tW", 0, 4), A("tW", 4, 8), O.not_equal)
        tt(A("q2"), A("q1"), A("isl"), O.mult)
        ts(A("q1"), A("q2"), 0.0, O.is_equal)
        tt(A("q3"), A("q1"), A("dW"), O.mult)
        tt(A("q1"), A("q2"), A("q3"), O.add)
        cp(A("Q%d" % t, QG + 512, QG + 576), IX(A("Q%d" % t, QG, QG + 512), A("OFC")))

    def cut511():
        cp(A("c511"), A("B5", 511, 512))
        mm(A("B7", 0, 1), A("TriB"), A("c511"))
        act(A("bs"), A("B7", 0, 1), F.Copy)
        act(A("B7"), A("B5"), F.Identity, A("bs"))

    def consume(t):
        tt(A("x0c"), A("x0c"), A("B7"), O.max)
        if t < RO - 1:
            dma("y", A("X", 0, 8192, 1, 0, 128, 16), A("x0c"))
        act(A("SG", t * 512, t * 512 + 512), A("x0c"), F.Sign, A("bB"))

    def merge(t):
        Q = "Q%d" % t
        nP, dP, nT, d2, d3 = A(Q, 64, 65), A(Q, 65, 66), A(Q, 200, 201), A(Q, 201, 202), A(Q, 202, 203)
        ts(A("mi", 0, 32), A("iW"), nP, O.is_ge, dP, O.mult)
        tt(A("mi", 32, 64), A("mi", 0, 32), A("iW"), O.add)
        tt(A("sN", 0, 1), nP, nT, O.add)
        tt(A("sN", 1, 2), A("sN", 0, 1), nT, O.add)
        ts(A("A1"), A("sN", 1, 2), -1.0, O.add)
        ts(A("OFD"), A("q1"), A("A1"), O.add)
        sct(A("Dw"), A("OFD"), A("i64b"))
        scan(A("DS"), A("Dw", 0, 512), A("Dw", 0, 512), 0.0, O.max, O.max)
        for r in range(16):
            mm(A("B3", 0, 32), A("Lsel", r * 128, r * 128 + 128), A("DS", r, 512, 16), r == 0, r == 15)
        cut511()
        ts(A("mi", 64, 96), A("iW"), A("sN", 0, 1), O.is_ge, d2, O.mult)
        ts(A("mi", 96, 128), A("iW"), A("sN", 1, 2), O.is_ge, d3, O.mult)
        tt(A("mi", 128, 160), A("mi", 32, 64), A("mi", 64, 96), O.add)
        tt(A("mi", 160, 192), A("mi", 128, 160), A("mi", 96, 128), O.add)
        tt(A("mi", 0, 32), A("B3", 0, 32), A("mi", 160, 192), O.add)
        cp(A("MI"), A("mi", 0, 32))
        for c in range(2):
            o = A("Gn", 256 * c, 256 * c + 256) if t == RO - 1 else A("Q%d" % (t + 1), QG + 256 * c, QG + 256 * c + 256)
            cp(o, IX(A(Q), A("MI", 16 * c, 16 * c + 16)))
        if t < RO - 1:
            iota(A("Dw"), [[0, DW]], 0, 0)

    def reverse(t):
        for c in range(4):
            mm(A("B6", c * 128, c * 128 + 128), A("SG", t * 512 + c * 128, t * 512 + c * 128 + 128), A("Pm"))
        act(A("RV1"), A("B6"), F.Copy)
        for c in range(4):
            mm(A("B5", (3 - c) * 128, (3 - c) * 128 + 128), A("RV1", c * 128, c * 128 + 128), A("Jm"))

    def utable(first):
        tt(A("okl"), A("B5"), A("i512") if first else A("okl"), O.min)
        scan(A("oks"), A("okl"), A("okl"), -16384.0, O.max, O.max)
        ts(A("tot"), A("oks", 511, 512), A("b512"), O.add)
        ts(A("dg"), A("idf"), A("tot"), O.mult)
        mm(A("B7", 0, 128), A("onef", 0, 128), A("dg"))

    def utable2():
        tt(A("cmx"), A("B7", 0, 128), A("cm"), O.mult)
        run("v", [A("cry")], [A("cmx")], lambda: V.tensor_reduce(A("cry")[0], A("cmx")[0], AxisListType.X, O.max))
        ts(A("Ut"), A("oks"), A("b512"), O.add, A("cry"), O.max)
        dma("y", A("Urep", 0, 8192, 1, 0, 128, 16), A("Ut"))

    for t in range(RO):
        if t == 0:
            consts0()
        else:
            consume(t - 1)
        p1a(t, 0)
        reps0(t)
        p1a(t, 1)
        p1b(0)
        lists(0)
        lists2(0)
        p1b(1)
        lists(1)
        reps1(t)
        if t == 0:
            consts1()
            consts2()
            reverse(4)
        else:
            reverse(t - 1)
        patterns(0)
        if t == 0:
            lists2(1)
            consts3()
        gather(0, 0, 4)
        if t > 0:
            lists2(1)
        patterns(1)
        act(A("UU", 0, 64, 2), A("UF", 16, 48), F.Copy, None, 64.0)
        act(A("UU", 1, 64, 2), A("UF", 16, 48), F.Copy)
        gather(0, 4, 8)
        sgather(12, "B3", 0)
        gather(0, 8, 12)
        sgather2(12, "B3")
        utable(t == 0)
        gather(0, 12, 16, True)
        sgather(14, "B4", 1)
        gather(1, 0, 4)
        sgather2(14, "B4")
        utable2()
        gather(1, 4, 8)
        gather(1, 8, 10)
        gather(1, 10, 11)
        gather(1, 11, 12, True)
        if t < RO - 1:
            weights(t + 1)
        lowest(0)
        lowest(1)
        decode()
        choose()
        resolve()
        give(t)
        order(t)
        merge(t)
    dma("y", (T.yg[:, :], []), A("Gn"))
    consume(RO - 1)
    for t in range(RO):
        mm(A("B5"), A("idb"), A("SG", t * 512, t * 512 + 512), t == 0, t == RO - 1)
    ts(A("Yt"), A("B5"), -0.5, O.mult, 3.0, O.add)
    ts(A("Yu"), A("B5"), -3.0, O.is_ge)
    tt(A("Yt"), A("Yt"), A("Yu"), O.mult)
    dma("y", (T.yc[:, :], []), A("Yt"))
    for s in count:
        if known["g"].get(s, 0) < count[s]:
            g.wait_ge(T.sem[s], count[s])
